import numpy as np
import ml_dtypes


def mxq(x, axis, fmt="e4m3"):
    dtype, down = {"e4m3": (ml_dtypes.float8_e4m3fn, 7), "e5m2": (ml_dtypes.float8_e5m2, 14)}[fmt]
    v = np.moveaxis(np.asarray(x, np.float32).astype(ml_dtypes.bfloat16).astype(np.float64), axis, -1)
    blocks = v.reshape(v.shape[:-1] + (-1, 32))
    amax = np.abs(blocks).max(-1, keepdims=True)
    byte = np.maximum(np.where(amax > 0, np.frexp(amax)[1] - 1 + 127, 0) - down, 1)
    scale = np.exp2(byte - 127.0)
    codes = (blocks / scale).astype(np.float32).astype(dtype).astype(np.float64)
    return np.moveaxis((codes * scale).reshape(v.shape), -1, axis)


WIDE = False


def mx_kscale(k):
    if not WIDE:
        return np.ones(k)
    levels = np.array([10, -10, 5, -5, 0])
    if k % 512:
        return np.exp2(np.random.permutation(np.resize(levels, k // 32))).repeat(32)
    a = np.empty((k // 512, 16))
    for p in range(k // 512):
        a[p, :8] = np.random.permutation(np.resize(levels, 8))
        for g in range(8):
            far = levels[np.abs(levels - a[p, g]) >= 10]
            a[p, g + 8] = far[np.random.randint(len(far))]
    return np.exp2(a.ravel()).repeat(32)


def f64(x):
    return np.asarray(x).astype(np.float64)


def striped(idx):
    return np.tile(idx.reshape(-1, 16).T, (8, 1)).astype(np.uint16)


def unstriped(offs):
    return offs[:16].T.reshape(-1).astype(np.int64)


def striped8(idx):
    return np.concatenate([x.reshape(-1, 16).T for x in idx]).astype(np.uint16)


def runs(offs, k):
    lists = np.stack([offs[16 * r : 16 * r + 16].T.reshape(-1) for r in range(8)]).astype(np.int64)
    return lists[np.arange(k) % 512 // 64]


def pack_weight(w):
    k, n = w.shape
    w = f64(np.asarray(w, np.float32).astype(ml_dtypes.bfloat16)).reshape(k // 32, 32, n)
    amax = np.abs(w).max(1)
    byte = np.clip(np.where(amax > 0, np.frexp(amax)[1] - 1 + 127 - 7, 1), 1, 254)
    scaled = (w * np.exp2(127.0 - byte)[:, None, :]).reshape(k, n).astype(np.float32)
    words = np.ascontiguousarray(scaled.reshape(k // 512, 128, 4, n).transpose(0, 1, 3, 2)).astype(ml_dtypes.float8_e4m3fn).view(np.uint8)
    return words, np.ascontiguousarray(byte.astype(np.uint8).reshape(k // 512, 16, n))


def unpack_weight(words, scales):
    g, p, n, _ = words.shape
    vals = np.ascontiguousarray(words).view(ml_dtypes.float8_e4m3fn).astype(np.float64) * np.repeat(np.exp2(scales.astype(np.float64) - 127.0), 8, axis=1)[..., None]
    return vals.transpose(0, 1, 3, 2).reshape(g * 512, n)


E2M1 = np.array([0.0, 0.5, 1.0, 1.5, 2.0, 3.0, 4.0, 6.0, -0.0, -0.5, -1.0, -1.5, -2.0, -3.0, -4.0, -6.0])


def pack_fp4(w):
    k, n = w.shape
    w = f64(np.asarray(w, np.float32).astype(ml_dtypes.bfloat16)).reshape(k // 32, 32, n)
    amax = np.abs(w).max(1)
    mant, ex = np.frexp(amax / 6.0)
    byte = np.clip(np.where(amax > 0, np.where(mant > 0.5, ex, ex - 1) + 127, 1), 1, 254)
    scaled = (w * np.exp2(127.0 - byte)[:, None, :]).reshape(k, n).astype(np.float32)
    c = np.ascontiguousarray(scaled.reshape(k // 512, 128, 4, n).transpose(0, 1, 3, 2)).astype(ml_dtypes.float4_e2m1fn).view(np.uint8) & 0xF
    words = (c[..., 0::2] | (c[..., 1::2] << 4)).reshape(k // 512, 128, 2 * n)
    return np.ascontiguousarray(words), np.ascontiguousarray(byte.astype(np.uint8).reshape(k // 512, 16, n))


def unpack_fp4(words, scales):
    g, _, n = scales.shape
    words = np.ascontiguousarray(words).reshape(g, 128, n, 2)
    nib = np.empty((g, 128, n, 4), np.uint8)
    nib[..., 0::2] = words & 0xF
    nib[..., 1::2] = words >> 4
    vals = E2M1[nib] * np.repeat(np.exp2(scales.astype(np.float64) - 127.0), 8, axis=1)[..., None]
    return vals.transpose(0, 1, 3, 2).reshape(g * 512, n)


def planes(y):
    n, m = y.shape
    v = y.astype(np.float32).astype(ml_dtypes.bfloat16).astype(np.float64).reshape(n // 32, 32, m)
    top = np.abs(v).max(1)
    byte = np.clip(np.where(top > 0, np.frexp(top)[1] - 1 + 127 - 7, 1), 1, 254)
    codes = (v * np.exp2(127.0 - byte)[:, None, :]).reshape(n, m).astype(np.float32).astype(ml_dtypes.float8_e4m3fn).view(np.uint8)
    words = codes.reshape(n // 512, 128, 4, m).transpose(0, 1, 3, 2)
    return np.ascontiguousarray(words), np.ascontiguousarray(byte.astype(np.uint8).reshape(n // 512, 16, m))


K, T, S, N, H, U = 512, 2048, 512, 512, 512, 1024


def setup_inputs():
    n = np.random.standard_normal
    s = mx_kscale(K)[:, None]
    u = mx_kscale(H)
    packed_xT = pack_weight(n((K, T)) * s)
    packed_w1 = pack_fp4(n((K, H)) / np.sqrt(K) / s)
    packed_w2 = pack_fp4(n((H, N)) / np.sqrt(H) / u[:, None])
    return {
        "x_words": packed_xT[0],
        "x_scales": packed_xT[1],
        "w1_words": packed_w1[0],
        "w1_scales": packed_w1[1],
        "gn": (np.random.uniform(0.5, 1.5, (H, 1)) * u[:, None]).astype(np.float32),
        "w2_words": packed_w2[0],
        "w2_scales": packed_w2[1],
        "pg": n((N, U)).astype(np.float32),
        "offs": striped(np.random.permutation(T)[:S]),
        "n1": striped8(np.stack([np.random.permutation(S) for _ in range(8)])),
        "slot": striped8(np.stack([np.random.permutation(U)[:S] for _ in range(8)])),
    }


def reference(x_words, x_scales, w1_words, w1_scales, gn, w2_words, w2_scales, pg, offs, n1, slot):
    xq = unpack_weight(x_words, x_scales)[:, unstriped(offs)]
    y = unpack_fp4(w1_words, w1_scales).T @ xq
    pw = (y) ** 2
    z = f64(gn) * (y * (np.exp(-0.5 * (pw[np.arange(H)[:, None], runs(n1, H)]))))
    h = unpack_fp4(w2_words, w2_scales).T @ mxq(z, 0, "e4m3")
    nw = f64(pg)[np.arange(N)[:, None], runs(slot, N)] + 0.5 * (np.tanh(h - (f64(pg)[np.arange(N)[:, None], runs(slot, N)])))
    out = f64(pg).copy()
    out[np.arange(N)[:, None], runs(slot, N)] = nw
    return (out,) + planes(out)

@@ -1,0 +1,189 @@
+from contextlib import ExitStack
+
+import concourse.mybir as mybir
+
+K, T, S, N, H, U = 512, 2048, 512, 512, 512, 1024
+FLOPS = 2 * K * H * S + 2 * H * N * S
+
+F32 = mybir.dt.float32
+BF16 = mybir.dt.bfloat16
+I32 = mybir.dt.int32
+U32 = mybir.dt.uint32
+U16 = mybir.dt.uint16
+U8 = mybir.dt.uint8
+FP8X4 = mybir.dt.float8_e4m3fn_x4
+FP4X4 = mybir.dt.float4_e2m1fn_x4
+ACT = mybir.ActivationFunctionType
+ALU = mybir.AluOpType
+
+P = 128
+PACK = 4
+HALF = S // 2
+ORDER = (2, 0, 1, 3)
+
+
+def load_scale_rows(queue, tile, rows):
+    for q in range(4):
+        queue.dma_start(out=tile[32 * q : 32 * q + 4, :].bitcast(I32), in_=rows[4 * q : 4 * q + 4, :].bitcast(I32))
+
+
+def tile_picked_masktrack_none_po_kernel(tc, x_words, x_scales, w1_words, w1_scales, gn, w2_words, w2_scales, pg, offs, n1, slot, out_0, out_1, out_2):
+    nc = tc.nc
+    with ExitStack() as ctx:
+        keep = ctx.enter_context(tc.tile_pool(name="keep", bufs=1))
+        psum = ctx.enter_context(tc.psum_pool(name="psum", bufs=1))
+
+        offs_sb = keep.tile([P, S // 16], U16)
+        n1_sb = keep.tile([P, S // 16], U16)
+        slot_sb = keep.tile([P, S // 16], U16)
+        xw = keep.tile([P, T], I32, align_bytes=64)
+        xs = keep.tile([P, T], U8, align_bytes=64)
+        w1w = keep.tile([P, 2 * H], U8, align_bytes=64)
+        w1s = keep.tile([P, H], U8, align_bytes=64)
+        w2w = keep.tile([P, 2 * N], U8, align_bytes=64)
+        w2s = keep.tile([P, N], U8, align_bytes=64)
+        gain = keep.tile([P, PACK], F32)
+        page = [keep.tile([P, U], F32, name=f"page{t}") for t in range(PACK)]
+
+        nc.gpsimd.memset(xs[:].bitcast(I32), 0)
+        nc.vector.memset(w1s[:].bitcast(I32), 0)
+        nc.vector.memset(w2s[:].bitcast(I32), 0)
+
+        pg_rows = pg.rearrange("(p t) w -> p t w", t=PACK)
+        nc.sync.dma_start(offs_sb[:], offs)
+        nc.sync.dma_start(out=w1w[:].bitcast(I32), in_=w1_words[0].bitcast(I32))
+        load_scale_rows(nc.sync, xs, x_scales[0])
+        nc.sync.dma_start(out=xw[:], in_=x_words[0].rearrange("p n t -> p (n t)").bitcast(I32))
+        load_scale_rows(nc.sync, w1s, w1_scales[0])
+        nc.sync.dma_start(slot_sb[:], slot)
+        nc.sync.dma_start(out=page[ORDER[0]][:], in_=pg_rows[:, ORDER[0], :])
+        nc.sync.dma_start(n1_sb[:], n1)
+        nc.sync.dma_start(out=w2w[:].bitcast(I32), in_=w2_words[0].bitcast(I32))
+        load_scale_rows(nc.sync, w2s, w2_scales[0])
+        nc.sync.dma_start(out=gain[:], in_=gn.rearrange("(p t) o -> p (t o)", t=PACK))
+        for t in ORDER[1:]:
+            nc.sync.dma_start(out=page[t][:], in_=pg_rows[:, t, :])
+
+        def deal_words(words, name):
+            dealt = keep.tile([P, 2 * H], U8, align_bytes=64, name=name)
+            nc.vector.tensor_copy(
+                out=dealt[:].rearrange("p (t m b) -> p t m b", t=PACK, b=2),
+                in_=words[:].rearrange("p (m t b) -> p t m b", t=PACK, b=2),
+            )
+            return dealt
+
+        def deal_scales(scales, name):
+            dealt = keep.tile([P, H], U8, align_bytes=64, name=name)
+            nc.vector.tensor_copy(
+                out=dealt[:].rearrange("p (t m) -> p t m", t=PACK),
+                in_=scales[:].rearrange("p (m t) -> p t m", t=PACK),
+            )
+            return dealt
+
+        def lists(tile, lo, hi):
+            return tile[:, lo // 16 : hi // 16]
+
+        xg_w = keep.tile([P, S], I32, align_bytes=64)
+        xg_s = keep.tile([P, S], U8, align_bytes=64)
+        w1dw = deal_words(w1w, "w1dw")
+        nc.vector.tensor_copy(xg_s[:], xs[:].indirect(offs_sb[:]))
+        nc.vector.tensor_copy(xg_w[:].bitcast(U32), xw[:].bitcast(U32).indirect(offs_sb[:]))
+        w1ds = deal_scales(w1s, "w1ds")
+
+        y = [psum.tile([P, S], F32, name=f"y{t}") for t in range(PACK)]
+        pw = [keep.tile([P, S], F32, name=f"pw{t}") for t in range(PACK)]
+        for t in range(PACK):
+            nc.tensor.matmul_mx(
+                out=y[t][:],
+                lhsT=w1dw[:, 2 * P * t : 2 * P * (t + 1)].bitcast(FP4X4),
+                lhsT_scale=w1ds[:, P * t : P * (t + 1)],
+                rhs=xg_w[:].bitcast(FP8X4),
+                rhs_scale=xg_s[:],
+                start=True,
+                stop=True,
+            )
+            nc.scalar.activation(pw[t][:], y[t][:], ACT.Square)
+
+        old = [keep.tile([P, S], F32, name=f"old{t}") for t in range(PACK)]
+        nc.vector.tensor_copy(old[ORDER[0]][:], page[ORDER[0]][:].indirect(slot_sb[:]))
+        w2dw = deal_words(w2w, "w2dw")
+        w2ds = deal_scales(w2s, "w2ds")
+        for t in ORDER[1:]:
+            nc.vector.tensor_copy(old[t][:], page[t][:].indirect(slot_sb[:]))
+
+        h = [psum.tile([P, S], F32, name=f"h{t}") for t in range(PACK)]
+        diff = [keep.tile([P, S], F32, name=f"diff{t}") for t in range(PACK)]
+        th = [keep.tile([P, S], F32, name=f"th{t}") for t in range(PACK)]
+        step = {t: keep.tile([P, S], F32, name=f"step{t}", tag=f"step{t}") for t in ORDER[:3]}
+
+        def move(t, lo, hi, halve=True):
+            nc.vector.tensor_tensor(diff[t][:, lo:hi], h[t][:, lo:hi], old[t][:, lo:hi], ALU.subtract)
+            nc.scalar.activation(th[t][:, lo:hi], diff[t][:, lo:hi], ACT.Tanh)
+            if halve:
+                nc.scalar.activation(step[t][:, lo:hi], th[t][:, lo:hi], ACT.Copy, scale=0.5)
+
+        def put(t, lo, hi):
+            nc.vector.tensor_tensor(page[t][:].indirect(lists(slot_sb, lo, hi)), old[t][:, lo:hi], step[t][:, lo:hi], ALU.add)
+
+        for half in range(2):
+            lo, hi = half * HALF, (half + 1) * HALF
+            mask = keep.tile([P, PACK, HALF], F32, name=f"mask{half}")
+            z = keep.tile([P, PACK, HALF], BF16, name=f"z{half}", tag="z")
+            z4 = keep.tile([P, HALF * PACK], BF16, align_bytes=64, name=f"z4{half}")
+            zw = keep.tile([P, HALF], I32, align_bytes=64, name=f"zw{half}")
+            zs = keep.tile([P, HALF], U8, align_bytes=64, name=f"zs{half}")
+            for t in range(PACK):
+                nc.scalar.activation(mask[:, t, :], pw[t][:].indirect(lists(n1_sb, lo, hi)), ACT.Exp, scale=-0.5)
+                nc.vector.scalar_tensor_tensor(z[:, t, :], y[t][:, lo:hi], gain[:, t : t + 1], mask[:, t, :], ALU.mult, ALU.mult)
+            nc.vector.tensor_copy(
+                out=z4[:].rearrange("p (c i t) -> p c t i", i=4, t=PACK),
+                in_=z[:].rearrange("p t (c i) -> p c t i", i=4),
+            )
+            nc.vector.quantize_mx(out=zw[:].bitcast(FP8X4), scales=zs[:], in_=z4[:])
+            for t in ORDER:
+                nc.tensor.matmul_mx(
+                    out=h[t][:, lo:hi],
+                    lhsT=w2dw[:, 2 * P * t : 2 * P * (t + 1)].bitcast(FP4X4),
+                    lhsT_scale=w2ds[:, P * t : P * (t + 1)],
+                    rhs=zw[:].bitcast(FP8X4),
+                    rhs_scale=zs[:],
+                    start=True,
+                    stop=True,
+                )
+            if half == 1:
+                put(ORDER[0], 0, HALF)
+            move(ORDER[0], lo, hi)
+
+        out_rows = out_0.rearrange("(p t) w -> p t w", t=PACK)
+        cut = U // 2
+        o4 = [keep.tile([P, cut, PACK], BF16, align_bytes=64, name=f"o4{side}") for side in range(2)]
+        ow = keep.tile([P, U], I32, align_bytes=64)
+        osc = keep.tile([P, U], U8, align_bytes=64)
+
+        def hand_out(t, left_copy):
+            nc.sync.dma_start(out=out_rows[:, t, :], in_=page[t][:])
+            left_copy(out=o4[0][:, :, t], in_=page[t][:, :cut])
+            nc.scalar.copy(out=o4[1][:, :, t], in_=page[t][:, cut:])
+
+        a, b, c, d = ORDER
+        move(b, 0, S)
+        move(c, 0, S)
+        move(d, 0, S, halve=False)
+        put(a, HALF, S)
+        hand_out(a, nc.scalar.copy)
+        step[d] = keep.tile([P, S], F32, name="step_last", tag=f"step{a}")
+        nc.scalar.activation(step[d][:], th[d][:], ACT.Copy, scale=0.5)
+        for t in (b, c):
+            put(t, 0, S)
+            hand_out(t, nc.scalar.copy)
+        put(d, 0, S)
+        hand_out(d, nc.vector.tensor_copy)
+        words_out = out_1[0].rearrange("p n t -> p (n t)").bitcast(I32)
+        for side in range(2):
+            lo, hi = side * cut, (side + 1) * cut
+            nc.vector.quantize_mx(
+                out=ow[:, lo:hi].bitcast(FP8X4), scales=osc[:, lo:hi], in_=o4[side][:].rearrange("p w t -> p (w t)")
+            )
+            nc.sync.dma_start(out=words_out[:, lo:hi], in_=ow[:, lo:hi])
+        for q in range(4):
+            nc.scalar.dma_start(out=out_2[0][4 * q : 4 * q + 4, :].bitcast(I32), in_=osc[32 * q : 32 * q + 4, :].bitcast(I32))

@@ -19,6 +19,7 @@ ALU = mybir.AluOpType
 P = 128
 PACK = 4
 HALF = S // 2
+X_CUT = 768
 ORDER = (2, 0, 1, 3)
 
 
@@ -39,30 +40,33 @@ def tile_picked_masktrack_none_po_kernel(tc, x_words, x_scales, w1_words, w1_sca
         xw = keep.tile([P, T], I32, align_bytes=64)
         xs = keep.tile([P, T], U8, align_bytes=64)
         w1w = keep.tile([P, 2 * H], U8, align_bytes=64)
-        w1s = keep.tile([P, H], U8, align_bytes=64)
-        w2w = keep.tile([P, 2 * N], U8, align_bytes=64)
+        w1s = keep.tile([P, H], U8, align_bytes=64, tag="w1s")
+        w2w = keep.tile([P, 2 * N], U8, align_bytes=64, tag="w2w")
         w2s = keep.tile([P, N], U8, align_bytes=64)
         gain = keep.tile([P, PACK], F32)
         page = [keep.tile([P, U], F32, name=f"page{t}") for t in range(PACK)]
 
-        nc.gpsimd.memset(xs[:].bitcast(I32), 0)
+        nc.vector.memset(xs[:].bitcast(I32), 0)
         nc.vector.memset(w1s[:].bitcast(I32), 0)
-        nc.vector.memset(w2s[:].bitcast(I32), 0)
+        nc.gpsimd.memset(w2s[:].bitcast(I32), 0)
 
         pg_rows = pg.rearrange("(p t) w -> p t w", t=PACK)
         nc.sync.dma_start(offs_sb[:], offs)
         nc.sync.dma_start(out=w1w[:].bitcast(I32), in_=w1_words[0].bitcast(I32))
+        x_in = x_words[0].rearrange("p n t -> p (n t)").bitcast(I32)
+        nc.sync.dma_start(out=xw[:, :X_CUT], in_=x_in[:, :X_CUT])
         load_scale_rows(nc.sync, xs, x_scales[0])
-        nc.sync.dma_start(out=xw[:], in_=x_words[0].rearrange("p n t -> p (n t)").bitcast(I32))
-        load_scale_rows(nc.sync, w1s, w1_scales[0])
-        nc.sync.dma_start(slot_sb[:], slot)
+        nc.sync.dma_start(out=xw[:, X_CUT:], in_=x_in[:, X_CUT:])
         nc.sync.dma_start(out=page[ORDER[0]][:], in_=pg_rows[:, ORDER[0], :])
+        nc.sync.dma_start(slot_sb[:], slot)
+        load_scale_rows(nc.sync, w1s, w1_scales[0])
+        for t in ORDER[1:3]:
+            nc.sync.dma_start(out=page[t][:], in_=pg_rows[:, t, :])
         nc.sync.dma_start(n1_sb[:], n1)
         nc.sync.dma_start(out=w2w[:].bitcast(I32), in_=w2_words[0].bitcast(I32))
-        load_scale_rows(nc.sync, w2s, w2_scales[0])
-        nc.sync.dma_start(out=gain[:], in_=gn.rearrange("(p t) o -> p (t o)", t=PACK))
-        for t in ORDER[1:]:
-            nc.sync.dma_start(out=page[t][:], in_=pg_rows[:, t, :])
+        nc.sync.dma_start(out=page[ORDER[3]][:], in_=pg_rows[:, ORDER[3], :])
+        load_scale_rows(nc.gpsimd, w2s, w2_scales[0])
+        nc.gpsimd.dma_start(out=gain[:], in_=gn.rearrange("(p t) o -> p (t o)", t=PACK))
 
         def deal_words(words, name):
             dealt = keep.tile([P, 2 * H], U8, align_bytes=64, name=name)
@@ -72,8 +76,8 @@ def tile_picked_masktrack_none_po_kernel(tc, x_words, x_scales, w1_words, w1_sca
             )
             return dealt
 
-        def deal_scales(scales, name):
-            dealt = keep.tile([P, H], U8, align_bytes=64, name=name)
+        def deal_scales(scales, name, tag):
+            dealt = keep.tile([P, H], U8, align_bytes=64, name=name, tag=tag)
             nc.vector.tensor_copy(
                 out=dealt[:].rearrange("p (t m) -> p t m", t=PACK),
                 in_=scales[:].rearrange("p (m t) -> p t m", t=PACK),
@@ -88,9 +92,9 @@ def tile_picked_masktrack_none_po_kernel(tc, x_words, x_scales, w1_words, w1_sca
         w1dw = deal_words(w1w, "w1dw")
         nc.vector.tensor_copy(xg_s[:], xs[:].indirect(offs_sb[:]))
         nc.vector.tensor_copy(xg_w[:].bitcast(U32), xw[:].bitcast(U32).indirect(offs_sb[:]))
-        w1ds = deal_scales(w1s, "w1ds")
+        w1ds = deal_scales(w1s, "w1ds", "w1ds")
 
-        y = [psum.tile([P, S], F32, name=f"y{t}") for t in range(PACK)]
+        y = [psum.tile([P, S], F32, name=f"y{t}", tag=f"bank{t}") for t in range(PACK)]
         pw = [keep.tile([P, S], F32, name=f"pw{t}") for t in range(PACK)]
         for t in range(PACK):
             nc.tensor.matmul_mx(
@@ -104,45 +108,38 @@ def tile_picked_masktrack_none_po_kernel(tc, x_words, x_scales, w1_words, w1_sca
             )
             nc.scalar.activation(pw[t][:], y[t][:], ACT.Square)
 
-        old = [keep.tile([P, S], F32, name=f"old{t}") for t in range(PACK)]
-        nc.vector.tensor_copy(old[ORDER[0]][:], page[ORDER[0]][:].indirect(slot_sb[:]))
-        w2dw = deal_words(w2w, "w2dw")
-        w2ds = deal_scales(w2s, "w2ds")
-        for t in ORDER[1:]:
+        a, b, c, d = ORDER
+        old = {}
+
+        def fetch_old(t, tag):
+            old[t] = keep.tile([P, S], F32, align_bytes=64, name=f"old{t}", tag=tag)
             nc.vector.tensor_copy(old[t][:], page[t][:].indirect(slot_sb[:]))
 
-        h = [psum.tile([P, S], F32, name=f"h{t}") for t in range(PACK)]
-        diff = [keep.tile([P, S], F32, name=f"diff{t}") for t in range(PACK)]
-        th = [keep.tile([P, S], F32, name=f"th{t}") for t in range(PACK)]
-        step = {t: keep.tile([P, S], F32, name=f"step{t}", tag=f"step{t}") for t in ORDER[:3]}
+        for t in (a, b, c):
+            fetch_old(t, "w1s" if t == a else f"old{t}")
+        w2dw = deal_words(w2w, "w2dw")
+        w2ds = deal_scales(w2s, "w2ds", "w2w")
 
-        def move(t, lo, hi, halve=True):
-            nc.vector.tensor_tensor(diff[t][:, lo:hi], h[t][:, lo:hi], old[t][:, lo:hi], ALU.subtract)
-            nc.scalar.activation(th[t][:, lo:hi], diff[t][:, lo:hi], ACT.Tanh)
-            if halve:
-                nc.scalar.activation(step[t][:, lo:hi], th[t][:, lo:hi], ACT.Copy, scale=0.5)
-
-        def put(t, lo, hi):
-            nc.vector.tensor_tensor(page[t][:].indirect(lists(slot_sb, lo, hi)), old[t][:, lo:hi], step[t][:, lo:hi], ALU.add)
-
+        h = {}
         for half in range(2):
             lo, hi = half * HALF, (half + 1) * HALF
-            mask = keep.tile([P, PACK, HALF], F32, name=f"mask{half}")
-            z = keep.tile([P, PACK, HALF], BF16, name=f"z{half}", tag="z")
-            z4 = keep.tile([P, HALF * PACK], BF16, align_bytes=64, name=f"z4{half}")
+            mask = keep.tile([P, PACK, HALF], F32, align_bytes=64, name=f"mask{half}", tag=f"mask{half}")
+            z = keep.tile([P, PACK, HALF], BF16, name=f"z{half}")
+            z4 = keep.tile([P, HALF * PACK], BF16, align_bytes=64, name=f"z4{half}", tag=f"z4{half}")
             zw = keep.tile([P, HALF], I32, align_bytes=64, name=f"zw{half}")
             zs = keep.tile([P, HALF], U8, align_bytes=64, name=f"zs{half}")
             for t in range(PACK):
                 nc.scalar.activation(mask[:, t, :], pw[t][:].indirect(lists(n1_sb, lo, hi)), ACT.Exp, scale=-0.5)
                 nc.vector.scalar_tensor_tensor(z[:, t, :], y[t][:, lo:hi], gain[:, t : t + 1], mask[:, t, :], ALU.mult, ALU.mult)
-            nc.vector.tensor_copy(
+            (nc.vector.tensor_copy if half == 0 else nc.scalar.copy)(
                 out=z4[:].rearrange("p (c i t) -> p c t i", i=4, t=PACK),
                 in_=z[:].rearrange("p t (c i) -> p c t i", i=4),
             )
             nc.vector.quantize_mx(out=zw[:].bitcast(FP8X4), scales=zs[:], in_=z4[:])
             for t in ORDER:
+                h[t, half] = psum.tile([P, HALF], F32, name=f"h{t}{half}", tag=f"bank{t + 4 * (1 - half)}")
                 nc.tensor.matmul_mx(
-                    out=h[t][:, lo:hi],
+                    out=h[t, half][:],
                     lhsT=w2dw[:, 2 * P * t : 2 * P * (t + 1)].bitcast(FP4X4),
                     lhsT_scale=w2ds[:, P * t : P * (t + 1)],
                     rhs=zw[:].bitcast(FP8X4),
@@ -150,9 +147,32 @@ def tile_picked_masktrack_none_po_kernel(tc, x_words, x_scales, w1_words, w1_sca
                     start=True,
                     stop=True,
                 )
-            if half == 1:
-                put(ORDER[0], 0, HALF)
-            move(ORDER[0], lo, hi)
+        fetch_old(d, "z41")
+
+        diff = {t: keep.tile([P, S], F32, name=f"diff{t}") for t in ORDER}
+        step = {t: keep.tile([P, S], F32, name=f"step{t}") for t in ORDER}
+        th = {t: keep.tile([P, S], F32, name=f"th{t}") for t in (a, c, d)}
+        th[b] = th[a]
+
+        def subtract(t, half):
+            cols = slice(half * HALF, (half + 1) * HALF)
+            nc.vector.tensor_tensor(diff[t][:, cols], h[t, half][:], old[t][:, cols], ALU.subtract)
+
+        def squash(t, cols):
+            nc.scalar.activation(th[t][:, cols], diff[t][:, cols], ACT.Tanh)
+            nc.scalar.activation(step[t][:, cols], th[t][:, cols], ACT.Copy, scale=0.5)
+
+        for t in (a, b, c):
+            subtract(t, 0)
+        squash(a, slice(0, HALF))
+        subtract(a, 1)
+        squash(a, slice(HALF, S))
+        for t in (b, c):
+            subtract(t, 1)
+            squash(t, slice(0, S))
+        subtract(d, 0)
+        subtract(d, 1)
+        squash(d, slice(0, S))
 
         out_rows = out_0.rearrange("(p t) w -> p t w", t=PACK)
         cut = U // 2
@@ -160,24 +180,16 @@ def tile_picked_masktrack_none_po_kernel(tc, x_words, x_scales, w1_words, w1_sca
         ow = keep.tile([P, U], I32, align_bytes=64)
         osc = keep.tile([P, U], U8, align_bytes=64)
 
-        def hand_out(t, left_copy):
+        for t in ORDER:
+            nc.vector.tensor_tensor(page[t][:].indirect(slot_sb[:]), old[t][:], step[t][:], ALU.add)
             nc.sync.dma_start(out=out_rows[:, t, :], in_=page[t][:])
-            left_copy(out=o4[0][:, :, t], in_=page[t][:, :cut])
+            if t == a:
+                nc.scalar.copy(out=o4[0][:, :, 2:4], in_=page[t][:, :cut].unsqueeze(2).to_broadcast([P, cut, 2]))
+            elif t == d:
+                nc.vector.tensor_copy(out=o4[0][:, :, t], in_=page[t][:, :cut])
+            else:
+                nc.scalar.copy(out=o4[0][:, :, t], in_=page[t][:, :cut])
             nc.scalar.copy(out=o4[1][:, :, t], in_=page[t][:, cut:])
-
-        a, b, c, d = ORDER
-        move(b, 0, S)
-        move(c, 0, S)
-        move(d, 0, S, halve=False)
-        put(a, HALF, S)
-        hand_out(a, nc.scalar.copy)
-        step[d] = keep.tile([P, S], F32, name="step_last", tag=f"step{a}")
-        nc.scalar.activation(step[d][:], th[d][:], ACT.Copy, scale=0.5)
-        for t in (b, c):
-            put(t, 0, S)
-            hand_out(t, nc.scalar.copy)
-        put(d, 0, S)
-        hand_out(d, nc.vector.tensor_copy)
         words_out = out_1[0].rearrange("p n t -> p (n t)").bitcast(I32)
         for side in range(2):
             lo, hi = side * cut, (side + 1) * cut
@@ -186,4 +198,4 @@ def tile_picked_masktrack_none_po_kernel(tc, x_words, x_scales, w1_words, w1_sca
             )
             nc.sync.dma_start(out=words_out[:, lo:hi], in_=ow[:, lo:hi])
         for q in range(4):
-            nc.scalar.dma_start(out=out_2[0][4 * q : 4 * q + 4, :].bitcast(I32), in_=osc[32 * q : 32 * q + 4, :].bitcast(I32))
+            (nc.scalar if q < 2 else nc.sync).dma_start(out=out_2[0][4 * q : 4 * q + 4, :].bitcast(I32), in_=osc[32 * q : 32 * q + 4, :].bitcast(I32))

@@ -149,10 +149,9 @@ def tile_picked_masktrack_none_po_kernel(tc, x_words, x_scales, w1_words, w1_sca
                 )
         fetch_old(d, "z41")
 
-        diff = {t: keep.tile([P, S], F32, name=f"diff{t}") for t in ORDER}
+        diff = {t: keep.tile([P, S], F32, align_bytes=64, name=f"diff{t}", tag=f"diff{t}") for t in ORDER}
         step = {t: keep.tile([P, S], F32, name=f"step{t}") for t in ORDER}
-        th = {t: keep.tile([P, S], F32, name=f"th{t}") for t in (a, c, d)}
-        th[b] = th[a]
+        th = {t: keep.tile([P, S], F32, align_bytes=64, name=f"th{t}", tag=f"th{t}") for t in ORDER}
 
         def subtract(t, half):
             cols = slice(half * HALF, (half + 1) * HALF)
@@ -164,19 +163,18 @@ def tile_picked_masktrack_none_po_kernel(tc, x_words, x_scales, w1_words, w1_sca
 
         for t in (a, b, c):
             subtract(t, 0)
-        squash(a, slice(0, HALF))
-        subtract(a, 1)
-        squash(a, slice(HALF, S))
-        for t in (b, c):
+        for t in (a, b, c):
+            squash(t, slice(0, HALF))
+        for t in (a, b, c):
             subtract(t, 1)
-            squash(t, slice(0, S))
+            squash(t, slice(HALF, S))
         subtract(d, 0)
         subtract(d, 1)
         squash(d, slice(0, S))
 
         out_rows = out_0.rearrange("(p t) w -> p t w", t=PACK)
         cut = U // 2
-        o4 = [keep.tile([P, cut, PACK], BF16, align_bytes=64, name=f"o4{side}") for side in range(2)]
+        o4 = [keep.tile([P, cut, PACK], BF16, align_bytes=64, name=f"o4{side}", tag=tag) for side, tag in enumerate((f"th{d}", f"diff{d}"))]
         ow = keep.tile([P, U], I32, align_bytes=64)
         osc = keep.tile([P, U], U8, align_bytes=64)
 

@@ -20,6 +20,7 @@ P = 128
 PACK = 4
 HALF = S // 2
 X_CUT = 768
+Z_CUT = 128
 ORDER = (2, 0, 1, 3)
 
 
@@ -39,9 +40,8 @@ def tile_picked_masktrack_none_po_kernel(tc, x_words, x_scales, w1_words, w1_sca
         slot_sb = keep.tile([P, S // 16], U16)
         xw = keep.tile([P, T], I32, align_bytes=64)
         xs = keep.tile([P, T], U8, align_bytes=64)
-        w1w = keep.tile([P, 2 * H], U8, align_bytes=64)
+        w1w = keep.tile([P, 2 * H], U8, align_bytes=64, tag="raw_words")
         w1s = keep.tile([P, H], U8, align_bytes=64, tag="w1s")
-        w2w = keep.tile([P, 2 * N], U8, align_bytes=64, tag="w2w")
         w2s = keep.tile([P, N], U8, align_bytes=64)
         gain = keep.tile([P, PACK], F32)
         page = [keep.tile([P, U], F32, name=f"page{t}") for t in range(PACK)]
@@ -63,22 +63,21 @@ def tile_picked_masktrack_none_po_kernel(tc, x_words, x_scales, w1_words, w1_sca
         for t in ORDER[1:3]:
             nc.sync.dma_start(out=page[t][:], in_=pg_rows[:, t, :])
         nc.sync.dma_start(n1_sb[:], n1)
-        nc.sync.dma_start(out=w2w[:].bitcast(I32), in_=w2_words[0].bitcast(I32))
         nc.sync.dma_start(out=page[ORDER[3]][:], in_=pg_rows[:, ORDER[3], :])
         load_scale_rows(nc.gpsimd, w2s, w2_scales[0])
         nc.gpsimd.dma_start(out=gain[:], in_=gn.rearrange("(p t) o -> p (t o)", t=PACK))
 
-        def deal_words(words, name):
+        def deal_words(engine, words, name):
             dealt = keep.tile([P, 2 * H], U8, align_bytes=64, name=name)
-            nc.vector.tensor_copy(
+            engine.tensor_copy(
                 out=dealt[:].rearrange("p (t m b) -> p t m b", t=PACK, b=2),
                 in_=words[:].rearrange("p (m t b) -> p t m b", t=PACK, b=2),
             )
             return dealt
 
-        def deal_scales(scales, name, tag):
-            dealt = keep.tile([P, H], U8, align_bytes=64, name=name, tag=tag)
-            nc.vector.tensor_copy(
+        def deal_scales(engine, scales, name):
+            dealt = keep.tile([P, H], U8, align_bytes=64, name=name)
+            engine.tensor_copy(
                 out=dealt[:].rearrange("p (t m) -> p t m", t=PACK),
                 in_=scales[:].rearrange("p (m t) -> p t m", t=PACK),
             )
@@ -89,10 +88,12 @@ def tile_picked_masktrack_none_po_kernel(tc, x_words, x_scales, w1_words, w1_sca
 
         xg_w = keep.tile([P, S], I32, align_bytes=64)
         xg_s = keep.tile([P, S], U8, align_bytes=64)
-        w1dw = deal_words(w1w, "w1dw")
+        w1dw = deal_words(nc.vector, w1w, "w1dw")
+        w2w = keep.tile([P, 2 * N], U8, align_bytes=64, tag="raw_words")
+        nc.gpsimd.dma_start(out=w2w[:].bitcast(I32), in_=w2_words[0].bitcast(I32))
         nc.vector.tensor_copy(xg_s[:], xs[:].indirect(offs_sb[:]))
         nc.vector.tensor_copy(xg_w[:].bitcast(U32), xw[:].bitcast(U32).indirect(offs_sb[:]))
-        w1ds = deal_scales(w1s, "w1ds", "w1ds")
+        w1ds = deal_scales(nc.vector, w1s, "w1ds")
 
         y = [psum.tile([P, S], F32, name=f"y{t}", tag=f"bank{t}") for t in range(PACK)]
         pw = [keep.tile([P, S], F32, name=f"pw{t}") for t in range(PACK)]
@@ -115,26 +116,30 @@ def tile_picked_masktrack_none_po_kernel(tc, x_words, x_scales, w1_words, w1_sca
             old[t] = keep.tile([P, S], F32, align_bytes=64, name=f"old{t}", tag=tag)
             nc.vector.tensor_copy(old[t][:], page[t][:].indirect(slot_sb[:]))
 
-        for t in (a, b, c):
+        for t in ORDER:
             fetch_old(t, "w1s" if t == a else f"old{t}")
-        w2dw = deal_words(w2w, "w2dw")
-        w2ds = deal_scales(w2s, "w2ds", "w2w")
+        w2ds = deal_scales(nc.gpsimd, w2s, "w2ds")
+        w2dw = deal_words(nc.gpsimd, w2w, "w2dw")
 
         h = {}
+        z = keep.tile([P, PACK, HALF], BF16)
         for half in range(2):
             lo, hi = half * HALF, (half + 1) * HALF
             mask = keep.tile([P, PACK, HALF], F32, align_bytes=64, name=f"mask{half}", tag=f"mask{half}")
-            z = keep.tile([P, PACK, HALF], BF16, name=f"z{half}")
             z4 = keep.tile([P, HALF * PACK], BF16, align_bytes=64, name=f"z4{half}", tag=f"z4{half}")
             zw = keep.tile([P, HALF], I32, align_bytes=64, name=f"zw{half}")
             zs = keep.tile([P, HALF], U8, align_bytes=64, name=f"zs{half}")
             for t in range(PACK):
                 nc.scalar.activation(mask[:, t, :], pw[t][:].indirect(lists(n1_sb, lo, hi)), ACT.Exp, scale=-0.5)
                 nc.vector.scalar_tensor_tensor(z[:, t, :], y[t][:, lo:hi], gain[:, t : t + 1], mask[:, t, :], ALU.mult, ALU.mult)
-            (nc.vector.tensor_copy if half == 0 else nc.scalar.copy)(
-                out=z4[:].rearrange("p (c i t) -> p c t i", i=4, t=PACK),
-                in_=z[:].rearrange("p t (c i) -> p c t i", i=4),
-            )
+            shares = [(nc.vector.tensor_copy, 0, HALF)]
+            if half == 1:
+                shares = [(nc.vector.tensor_copy, 0, Z_CUT), (nc.scalar.copy, Z_CUT, HALF)]
+            for copy, c0, c1 in shares:
+                copy(
+                    out=z4[:, PACK * c0 : PACK * c1].rearrange("p (c i t) -> p c t i", i=4, t=PACK),
+                    in_=z[:, :, c0:c1].rearrange("p t (c i) -> p c t i", i=4),
+                )
             nc.vector.quantize_mx(out=zw[:].bitcast(FP8X4), scales=zs[:], in_=z4[:])
             for t in ORDER:
                 h[t, half] = psum.tile([P, HALF], F32, name=f"h{t}{half}", tag=f"bank{t + 4 * (1 - half)}")
@@ -147,7 +152,6 @@ def tile_picked_masktrack_none_po_kernel(tc, x_words, x_scales, w1_words, w1_sca
                     start=True,
                     stop=True,
                 )
-        fetch_old(d, "z41")
 
         diff = {t: keep.tile([P, S], F32, align_bytes=64, name=f"diff{t}", tag=f"diff{t}") for t in ORDER}
         step = {t: keep.tile([P, S], F32, name=f"step{t}") for t in ORDER}
@@ -161,16 +165,13 @@ def tile_picked_masktrack_none_po_kernel(tc, x_words, x_scales, w1_words, w1_sca
             nc.scalar.activation(th[t][:, cols], diff[t][:, cols], ACT.Tanh)
             nc.scalar.activation(step[t][:, cols], th[t][:, cols], ACT.Copy, scale=0.5)
 
-        for t in (a, b, c):
+        for t in ORDER:
             subtract(t, 0)
-        for t in (a, b, c):
+        for t in (a, b):
             squash(t, slice(0, HALF))
-        for t in (a, b, c):
+        for t in ORDER:
             subtract(t, 1)
-            squash(t, slice(HALF, S))
-        subtract(d, 0)
-        subtract(d, 1)
-        squash(d, slice(0, S))
+            squash(t, slice(HALF if t in (a, b) else 0, S))
 
         out_rows = out_0.rearrange("(p t) w -> p t w", t=PACK)
         cut = U // 2

from contextlib import ExitStack

import concourse.mybir as mybir

K, T, S, N, H, U = 512, 2048, 512, 512, 512, 1024
FLOPS = 2 * K * H * S + 2 * H * N * S

F32 = mybir.dt.float32
BF16 = mybir.dt.bfloat16
I32 = mybir.dt.int32
U32 = mybir.dt.uint32
U16 = mybir.dt.uint16
U8 = mybir.dt.uint8
FP8X4 = mybir.dt.float8_e4m3fn_x4
FP4X4 = mybir.dt.float4_e2m1fn_x4
ACT = mybir.ActivationFunctionType
ALU = mybir.AluOpType

P = 128
PACK = 4
HALF = S // 2
X_CUT = 768
Z_CUT = 128
ORDER = (2, 0, 1, 3)


def load_scale_rows(queue, tile, rows):
    for q in range(4):
        queue.dma_start(out=tile[32 * q : 32 * q + 4, :].bitcast(I32), in_=rows[4 * q : 4 * q + 4, :].bitcast(I32))


def tile_picked_masktrack_none_po_kernel(tc, x_words, x_scales, w1_words, w1_scales, gn, w2_words, w2_scales, pg, offs, n1, slot, out_0, out_1, out_2):
    nc = tc.nc
    with ExitStack() as ctx:
        keep = ctx.enter_context(tc.tile_pool(name="keep", bufs=1))
        psum = ctx.enter_context(tc.psum_pool(name="psum", bufs=1))

        offs_sb = keep.tile([P, S // 16], U16)
        n1_sb = keep.tile([P, S // 16], U16)
        slot_sb = keep.tile([P, S // 16], U16)
        xw = keep.tile([P, T], I32, align_bytes=64)
        xs = keep.tile([P, T], U8, align_bytes=64)
        w1w = keep.tile([P, 2 * H], U8, align_bytes=64, tag="raw_words")
        w1s = keep.tile([P, H], U8, align_bytes=64, tag="w1s")
        w2s = keep.tile([P, N], U8, align_bytes=64)
        gain = keep.tile([P, PACK], F32)
        page = [keep.tile([P, U], F32, name=f"page{t}") for t in range(PACK)]

        nc.vector.memset(xs[:].bitcast(I32), 0)
        nc.vector.memset(w1s[:].bitcast(I32), 0)
        nc.gpsimd.memset(w2s[:].bitcast(I32), 0)

        pg_rows = pg.rearrange("(p t) w -> p t w", t=PACK)
        nc.sync.dma_start(offs_sb[:], offs)
        nc.sync.dma_start(out=w1w[:].bitcast(I32), in_=w1_words[0].bitcast(I32))
        x_in = x_words[0].rearrange("p n t -> p (n t)").bitcast(I32)
        nc.sync.dma_start(out=xw[:, :X_CUT], in_=x_in[:, :X_CUT])
        load_scale_rows(nc.sync, xs, x_scales[0])
        nc.sync.dma_start(out=xw[:, X_CUT:], in_=x_in[:, X_CUT:])
        nc.sync.dma_start(out=page[ORDER[0]][:], in_=pg_rows[:, ORDER[0], :])
        nc.sync.dma_start(slot_sb[:], slot)
        load_scale_rows(nc.sync, w1s, w1_scales[0])
        for t in ORDER[1:3]:
            nc.sync.dma_start(out=page[t][:], in_=pg_rows[:, t, :])
        nc.sync.dma_start(n1_sb[:], n1)
        nc.sync.dma_start(out=page[ORDER[3]][:], in_=pg_rows[:, ORDER[3], :])
        load_scale_rows(nc.gpsimd, w2s, w2_scales[0])
        nc.gpsimd.dma_start(out=gain[:], in_=gn.rearrange("(p t) o -> p (t o)", t=PACK))

        def deal_words(engine, words, name):
            dealt = keep.tile([P, 2 * H], U8, align_bytes=64, name=name)
            engine.tensor_copy(
                out=dealt[:].rearrange("p (t m b) -> p t m b", t=PACK, b=2),
                in_=words[:].rearrange("p (m t b) -> p t m b", t=PACK, b=2),
            )
            return dealt

        def deal_scales(engine, scales, name):
            dealt = keep.tile([P, H], U8, align_bytes=64, name=name)
            engine.tensor_copy(
                out=dealt[:].rearrange("p (t m) -> p t m", t=PACK),
                in_=scales[:].rearrange("p (m t) -> p t m", t=PACK),
            )
            return dealt

        def lists(tile, lo, hi):
            return tile[:, lo // 16 : hi // 16]

        xg_w = keep.tile([P, S], I32, align_bytes=64)
        xg_s = keep.tile([P, S], U8, align_bytes=64)
        w1dw = deal_words(nc.vector, w1w, "w1dw")
        w2w = keep.tile([P, 2 * N], U8, align_bytes=64, tag="raw_words")
        nc.gpsimd.dma_start(out=w2w[:].bitcast(I32), in_=w2_words[0].bitcast(I32))
        nc.vector.tensor_copy(xg_s[:], xs[:].indirect(offs_sb[:]))
        nc.vector.tensor_copy(xg_w[:].bitcast(U32), xw[:].bitcast(U32).indirect(offs_sb[:]))
        w1ds = deal_scales(nc.vector, w1s, "w1ds")

        y = [psum.tile([P, S], F32, name=f"y{t}", tag=f"bank{t}") for t in range(PACK)]
        pw = [keep.tile([P, S], F32, name=f"pw{t}") for t in range(PACK)]
        for t in range(PACK):
            nc.tensor.matmul_mx(
                out=y[t][:],
                lhsT=w1dw[:, 2 * P * t : 2 * P * (t + 1)].bitcast(FP4X4),
                lhsT_scale=w1ds[:, P * t : P * (t + 1)],
                rhs=xg_w[:].bitcast(FP8X4),
                rhs_scale=xg_s[:],
                start=True,
                stop=True,
            )
            nc.scalar.activation(pw[t][:], y[t][:], ACT.Square)

        a, b, c, d = ORDER
        old = {}

        def fetch_old(t, tag):
            old[t] = keep.tile([P, S], F32, align_bytes=64, name=f"old{t}", tag=tag)
            nc.vector.tensor_copy(old[t][:], page[t][:].indirect(slot_sb[:]))

        for t in ORDER:
            fetch_old(t, "w1s" if t == a else f"old{t}")
        w2ds = deal_scales(nc.gpsimd, w2s, "w2ds")
        w2dw = deal_words(nc.gpsimd, w2w, "w2dw")

        h = {}
        z = keep.tile([P, PACK, HALF], BF16)
        for half in range(2):
            lo, hi = half * HALF, (half + 1) * HALF
            mask = keep.tile([P, PACK, HALF], F32, align_bytes=64, name=f"mask{half}", tag=f"mask{half}")
            z4 = keep.tile([P, HALF * PACK], BF16, align_bytes=64, name=f"z4{half}", tag=f"z4{half}")
            zw = keep.tile([P, HALF], I32, align_bytes=64, name=f"zw{half}")
            zs = keep.tile([P, HALF], U8, align_bytes=64, name=f"zs{half}")
            for t in range(PACK):
                nc.scalar.activation(mask[:, t, :], pw[t][:].indirect(lists(n1_sb, lo, hi)), ACT.Exp, scale=-0.5)
                nc.vector.scalar_tensor_tensor(z[:, t, :], y[t][:, lo:hi], gain[:, t : t + 1], mask[:, t, :], ALU.mult, ALU.mult)
            shares = [(nc.vector.tensor_copy, 0, HALF)]
            if half == 1:
                shares = [(nc.vector.tensor_copy, 0, Z_CUT), (nc.scalar.copy, Z_CUT, HALF)]
            for copy, c0, c1 in shares:
                copy(
                    out=z4[:, PACK * c0 : PACK * c1].rearrange("p (c i t) -> p c t i", i=4, t=PACK),
                    in_=z[:, :, c0:c1].rearrange("p t (c i) -> p c t i", i=4),
                )
            nc.vector.quantize_mx(out=zw[:].bitcast(FP8X4), scales=zs[:], in_=z4[:])
            for t in ORDER:
                h[t, half] = psum.tile([P, HALF], F32, name=f"h{t}{half}", tag=f"bank{t + 4 * (1 - half)}")
                nc.tensor.matmul_mx(
                    out=h[t, half][:],
                    lhsT=w2dw[:, 2 * P * t : 2 * P * (t + 1)].bitcast(FP4X4),
                    lhsT_scale=w2ds[:, P * t : P * (t + 1)],
                    rhs=zw[:].bitcast(FP8X4),
                    rhs_scale=zs[:],
                    start=True,
                    stop=True,
                )

        diff = {t: keep.tile([P, S], F32, align_bytes=64, name=f"diff{t}", tag=f"diff{t}") for t in ORDER}
        step = {t: keep.tile([P, S], F32, name=f"step{t}") for t in ORDER}
        th = {t: keep.tile([P, S], F32, align_bytes=64, name=f"th{t}", tag=f"th{t}") for t in ORDER}

        def subtract(t, half):
            cols = slice(half * HALF, (half + 1) * HALF)
            nc.vector.tensor_tensor(diff[t][:, cols], h[t, half][:], old[t][:, cols], ALU.subtract)

        def squash(t, cols):
            nc.scalar.activation(th[t][:, cols], diff[t][:, cols], ACT.Tanh)
            nc.scalar.activation(step[t][:, cols], th[t][:, cols], ACT.Copy, scale=0.5)

        for t in ORDER:
            subtract(t, 0)
        for t in (a, b):
            squash(t, slice(0, HALF))
        for t in ORDER:
            subtract(t, 1)
            squash(t, slice(HALF if t in (a, b) else 0, S))

        out_rows = out_0.rearrange("(p t) w -> p t w", t=PACK)
        cut = U // 2
        o4 = [keep.tile([P, cut, PACK], BF16, align_bytes=64, name=f"o4{side}", tag=tag) for side, tag in enumerate((f"th{d}", f"diff{d}"))]
        ow = keep.tile([P, U], I32, align_bytes=64)
        osc = keep.tile([P, U], U8, align_bytes=64)

        for t in ORDER:
            nc.vector.tensor_tensor(page[t][:].indirect(slot_sb[:]), old[t][:], step[t][:], ALU.add)
            nc.sync.dma_start(out=out_rows[:, t, :], in_=page[t][:])
            if t == a:
                nc.scalar.copy(out=o4[0][:, :, 2:4], in_=page[t][:, :cut].unsqueeze(2).to_broadcast([P, cut, 2]))
            elif t == d:
                nc.vector.tensor_copy(out=o4[0][:, :, t], in_=page[t][:, :cut])
            else:
                nc.scalar.copy(out=o4[0][:, :, t], in_=page[t][:, :cut])
            nc.scalar.copy(out=o4[1][:, :, t], in_=page[t][:, cut:])
        words_out = out_1[0].rearrange("p n t -> p (n t)").bitcast(I32)
        for side in range(2):
            lo, hi = side * cut, (side + 1) * cut
            nc.vector.quantize_mx(
                out=ow[:, lo:hi].bitcast(FP8X4), scales=osc[:, lo:hi], in_=o4[side][:].rearrange("p w t -> p (w t)")
            )
            nc.sync.dma_start(out=words_out[:, lo:hi], in_=ow[:, lo:hi])
        for q in range(4):
            (nc.scalar if q < 2 else nc.sync).dma_start(out=out_2[0][4 * q : 4 * q + 4, :].bitcast(I32), in_=osc[32 * q : 32 * q + 4, :].bitcast(I32))
